import numpy as np, ml_dtypes
CORES = [61,69,101,62,70,102]
N = 6
import mx_ref
NC, G = 512, 4
C = np.float32(0.0217)
BF = ml_dtypes.bfloat16
def cut(t, i, w=512):
    return t[:, w * i:w * i + w]
def tile(rs):
    return np.stack(rs, axis=2).reshape(128, -1).astype(BF)
def layer(w, X):
    out = []
    for i in range(G):
        for t in range(len(X)):
            p = mx_ref.matmul(mx_ref.quantize(cut(w, len(X) * i + t)), X[t])
            z = p if t == 0 else z + p
        out.append(z)
    return out
def act(Z):
    return [np.maximum(z, 0) * C for z in Z]
def setup_inputs(rng):
    def f(*shape):
        return mx_ref.flush((rng.standard_normal(shape, dtype=np.float32) * np.exp2(rng.integers(-2, 3, shape[:-1] + (1,)))).astype(BF))
    return {"s": f(N, 128, 4 * NC), "x": f(N, 128, 4 * NC), "w": f(N, 128, 2 * G * 512), "v": f(N, 128, 512)}
def setup_inputs_blocks(rng):
    d = setup_inputs(rng)
    for k in ("s", "x", "v"): d[k] = mx_ref.spread(d[k], rng, 4)
    for k in ("w",): d[k] = mx_ref.spread(d[k], rng, 1)
    return d
def setup_inputs_wide(rng):
    d = setup_inputs(rng)
    for k in ("s", "x", "v"): d[k] = mx_ref.flush((d[k].astype(np.float32) * np.exp2(rng.integers(-6, 7, (N, 1, 1))).astype(np.float32)).astype(BF))
    return d
def setup_inputs_zeros(rng):
    d = setup_inputs(rng); v = d["x"].reshape(N, 128, -1, 4).copy()
    v[np.broadcast_to((rng.random((N, 1, v.shape[2], 1)) < 0.33), v.shape)] = 0
    d["x"] = v.reshape(d["x"].shape)
    return d
def reference(s, x, w, v):
    q = mx_ref.quantize(s[0])
    y = np.zeros((N, 128, NC), np.float32)
    for r in range(N):
        q = mx_ref.quantize(tile(act(layer(w[r], [q, mx_ref.quantize(x[r])]))))
        y[r] = mx_ref.matmul(mx_ref.quantize(v[r]), q)
    return {"y": y}

@@ -1,0 +1,241 @@
+import numpy as np
+from concourse.mybir import dt, AluOpType, ActivationFunctionType
+
+SIM_CORES = 112
+NC, G = 512, 4
+WIDTHS = (128, 128, 128, 128)
+K = len(WIDTHS)
+OFFS = tuple(sum(WIDTHS[:c]) for c in range(K))
+CF = float(np.float32(0.0217))
+
+SCRATCH = {
+    "sb": ("sbuf", [128, 4 * NC], "bfloat16"),
+    "xb": ("sbuf", [128, 4 * NC], "bfloat16"),
+    "wb": ("sbuf", [128, 2 * G * 512], "bfloat16"),
+    "vb": ("sbuf", [128, 512], "bfloat16"),
+    "sq": ("sbuf", [128, NC], "float8_e4m3fn_x4"), "sp": ("sbuf", [128, NC], "uint8"),
+    "xq": ("sbuf", [128, NC], "float8_e4m3fn_x4"), "xp": ("sbuf", [128, NC], "uint8"),
+    "wq": ("sbuf", [128, 2 * G * 128], "float8_e4m3fn_x4"), "wp": ("sbuf", [128, 2 * G * 128], "uint8"),
+    "vq": ("sbuf", [128, 128], "float8_e4m3fn_x4"), "vp": ("sbuf", [128, 128], "uint8"),
+    "iq": ("sbuf", [128, NC], "float8_e4m3fn_x4"), "ip": ("sbuf", [128, NC], "uint8"),
+    "hb": ("sbuf", [128, 4 * NC], "bfloat16"),
+    "hq": ("sbuf", [128, NC], "float8_e4m3fn_x4"), "hp": ("sbuf", [128, NC], "uint8"),
+    "rq": ("sbuf", [128, NC], "float8_e4m3fn_x4"), "rp": ("sbuf", [128, NC], "uint8"),
+    "yb": ("sbuf", [128, NC], "float32"),
+    "ps": ("psum", [128, 8 * 512], "float32"),
+}
+SEMAPHORES = (["ls%d" % c for c in range(K)] + ["lx%d" % c for c in range(K)] + ["lw%d" % i for i in range(G)] + ["lv"]
+              + ["qz", "mm", "av", "ac", "hz", "yc", "yst", "sent"]
+              + ["arr%d" % c for c in range(K)] + ["relc%d" % c for c in range(K)] + ["relp%d" % c for c in range(K)])
+
+
+def engines(m):
+    return bin(m).count("1")
+
+
+def route(T, topo):
+    cores = list(T.cores)
+    hops = []
+    for src, dst in zip(cores, cores[1:]):
+        if topo.may_write(src, dst):
+            hops.append((src, dst, None, None))
+            continue
+        cand = [c for c in range(SIM_CORES)
+                if c != src and c != dst and topo.chip(c) == topo.chip(src) and topo.may_write(c, dst)]
+        cand.sort(key=lambda c: (topo.die(c) != topo.die(src), c not in cores, c))
+        hops.append((src, dst, cand[0], cand[min(1, len(cand) - 1)]))
+    return hops
+
+
+def rank_program(g, core, T, topo):
+    hops = route(T, topo)
+    rank = T.rank_of(core)
+    if rank is None and not any(core in (h[2], h[3]) for h in hops):
+        return
+    nranks = len(T.cores)
+    cnt, seen = {}, {}
+
+    def mark(ins, name, n=1):
+        cnt[name] = cnt.get(name, 0) + n
+        ins.then_inc(T.sem[name], n)
+        return (name, cnt[name])
+
+    def wait(q, qn, tok):
+        if seen.get((qn, tok[0]), 0) < tok[1]:
+            seen[(qn, tok[0])] = tok[1]
+            q.wait_ge(T.sem[tok[0]], tok[1])
+
+    hz = {}
+    if rank is not None:
+        PE, V, S, SY = g.tensor, g.vector, g.scalar, g.sync
+        first, last = rank == 0, rank == nranks - 1
+        ld, qz, mm, act_t, yc_t = {}, {}, {}, {}, {}
+        nld = [0]
+
+        def load(key, sem, buf, src, lo, hi):
+            q = (SY, S)[nld[0] % 2]
+            nld[0] += 1
+            ld[key] = mark(q.dma_start(buf[:, lo:hi], src[:, lo:hi]), sem, 16)
+
+        def quant(key, codes, plane, buf, lo, hi):
+            wait(V, "v", ld[key])
+            qz[key] = mark(V.quantize_mx(codes[:, lo:hi], plane[:, lo:hi], buf[:, 4 * lo:4 * hi]), "qz")
+
+        def span(c):
+            return OFFS[c], OFFS[c] + WIDTHS[c]
+
+        def ld_s(c):
+            load(("s", c), "ls%d" % c, T.sb, T.s, 4 * span(c)[0], 4 * span(c)[1])
+
+        def ld_x(c):
+            load(("x", c), "lx%d" % c, T.xb, T.x, 4 * span(c)[0], 4 * span(c)[1])
+
+        def bank(c, i):
+            lo = 512 * (G * (c % 2) + i)
+            return T.ps[:, lo:lo + WIDTHS[c]]
+
+        if first:
+            xkey, wkey = (lambda c: ("x", c)), (lambda i: ("w", i))
+            ld_s(0)
+            ld_x(0)
+            for i in range(G):
+                load(("w", i), "lw%d" % i, T.wb, T.w, 1024 * i, 1024 * i + 1024)
+            for c in range(1, K):
+                ld_s(c)
+                ld_x(c)
+            load("v", "lv", T.vb, T.v, 0, 512)
+            iq, ip = T.sq, T.sp
+        else:
+            xkey, wkey = (lambda c: ("x", 0)), (lambda i: ("w", i // 2))
+            for h in range(2):
+                load(("w", h), "lw%d" % h, T.wb, T.w, 2048 * h, 2048 * h + 2048)
+            load(("x", 0), "lx0", T.xb, T.x, 0, 4 * NC)
+            load("v", "lv", T.vb, T.v, 0, 512)
+            for h in range(2):
+                quant(("w", h), T.wq, T.wp, T.wb, 512 * h, 512 * h + 512)
+            quant(("x", 0), T.xq, T.xp, T.xb, 0, NC)
+            quant("v", T.vq, T.vp, T.vb, 0, 128)
+            iq, ip = T.iq, T.ip
+            src, dst, cv, pv = hops[rank - 1]
+            landed = engines(topo.mask(src if cv is None else cv, dst)) + engines(topo.mask(src if pv is None else pv, dst))
+
+        def mm_x(c, i):
+            a, b = span(c)
+            k = 128 * (2 * i + 1)
+            wait(PE, "pe", qz[wkey(i)])
+            wait(PE, "pe", qz[xkey(c)])
+            if c >= 2:
+                wait(PE, "pe", act_t[(c - 2, i)])
+                if (c - 2, i) in yc_t:
+                    wait(PE, "pe", yc_t[(c - 2, i)])
+            PE.matmul_mx(bank(c, i), T.wq[:, k:k + 128], T.wp[:, k:k + 128], T.xq[:, a:b], T.xp[:, a:b], True, False)
+
+        def mm_q(c, i):
+            a, b = span(c)
+            k = 128 * (2 * i)
+            if first:
+                wait(PE, "pe", qz[("s", c)])
+            else:
+                wait(PE, "pe", ("arr%d" % c, landed))
+            mm[(c, i)] = mark(PE.matmul_mx(bank(c, i), T.wq[:, k:k + 128], T.wp[:, k:k + 128],
+                                           iq[:, a:b], ip[:, a:b], False, True), "mm")
+
+        def act(c, i, on_vector):
+            a, b = span(c)
+            out = T.hb[:, 4 * a + i:4 * b:4]
+            if on_vector:
+                wait(V, "v", mm[(c, i)])
+                act_t[(c, i)] = mark(V.tensor_scalar(out, bank(c, i), 0.0, CF, AluOpType.max, AluOpType.mult), "av")
+            else:
+                wait(S, "s", mm[(c, i)])
+                act_t[(c, i)] = mark(S.activation(out, bank(c, i), ActivationFunctionType.Relu, scale=CF), "ac")
+
+        def pack(c):
+            a, b = span(c)
+            for i in range(G):
+                wait(V, "v", act_t[(c, i)])
+            hz[c] = mark(V.quantize_mx(T.hq[:, a:b], T.hp[:, a:b], T.hb[:, 4 * a:4 * b]), "hz")
+
+        def y_part(a, b, out, users):
+            wait(PE, "pe", qz["v"])
+            for u in users:
+                wait(PE, "pe", u)
+            t = mark(PE.matmul_mx(out, T.vq[:], T.vp[:], T.hq[:, a:b], T.hp[:, a:b], True, True), "mm")
+            wait(S, "s", t)
+            t = mark(S.activation(T.yb[:, a:b], out, ActivationFunctionType.Copy), "yc")
+            wait(SY, "sy", t)
+            mark(SY.dma_start(T.y[:, a:b], T.yb[:, a:b]), "yst", 16)
+            return t
+
+        if first:
+            quant(("s", 0), T.sq, T.sp, T.sb, *span(0))
+            quant(("x", 0), T.xq, T.xp, T.xb, *span(0))
+            for i in range(G):
+                quant(("w", i), T.wq, T.wp, T.wb, 256 * i, 256 * i + 256)
+                mm_x(0, i)
+                mm_q(0, i)
+                act(0, i, False)
+            pack(0)
+            for c in range(1, K + 1):
+                if c < K:
+                    quant(("s", c), T.sq, T.sp, T.sb, *span(c))
+                    quant(("x", c), T.xq, T.xp, T.xb, *span(c))
+                if c >= 2:
+                    pack(c - 1)
+                if c < K:
+                    for i in range(G):
+                        mm_x(c, i)
+                        mm_q(c, i)
+                        act(c, i, False)
+            quant("v", T.vq, T.vp, T.vb, 0, 128)
+        else:
+            for c in range(min(2, K)):
+                for i in range(G):
+                    mm_x(c, i)
+            later = []
+            for c in range(K):
+                for i in range(G):
+                    mm_q(c, i)
+                    act(c, i, i % 2 == 0)
+                for cc, ii in later:
+                    mm_x(cc, ii)
+                later = []
+                pack(c)
+                if c + 2 < K:
+                    for i in range(G):
+                        if last and i == 0:
+                            later.append((c + 2, i))
+                        else:
+                            mm_x(c + 2, i)
+                if last:
+                    yc_t[(c, 0)] = y_part(span(c)[0], span(c)[1], bank(c, 0), [hz[c], act_t[(c, 0)]])
+        if not last:
+            busy = [act_t[(c, 0)] for c in range(K) if c % 2 == 0]
+            y_part(0, NC, T.ps[:, 0:NC], [hz[K - 1], busy[-1]])
+        wait(SY, "sy", ("yst", cnt["yst"]))
+
+    def push(to, out_ap, in_ap, sem):
+        rid, pid = topo.addr(to)[:2]
+        m = topo.mask(core, to)
+        g.remote_dma(out_ap, in_ap, T.sem[sem], T.sem.sent, pid, rid, m)
+        cnt["sent"] = cnt.get("sent", 0) + engines(m)
+
+    for src, dst, cv, pv in hops:
+        for c in range(K):
+            a, b = OFFS[c], OFFS[c] + WIDTHS[c]
+            if core == src:
+                wait(g, "g", hz[c])
+                if cv is None:
+                    push(dst, T.iq[:, a:b].bitcast(dt.uint8), T.hq[:, a:b].bitcast(dt.uint8), "arr%d" % c)
+                    push(dst, T.ip[:, a:b], T.hp[:, a:b], "arr%d" % c)
+                else:
+                    push(cv, T.rq[:, a:b].bitcast(dt.uint8), T.hq[:, a:b].bitcast(dt.uint8), "relc%d" % c)
+                    push(pv, T.rp[:, a:b], T.hp[:, a:b], "relp%d" % c)
+            if core == cv:
+                wait(g, "g", ("relc%d" % c, engines(topo.mask(src, cv))))
+                push(dst, T.iq[:, a:b].bitcast(dt.uint8), T.rq[:, a:b].bitcast(dt.uint8), "arr%d" % c)
+            if core == pv:
+                wait(g, "g", ("relp%d" % c, engines(topo.mask(src, pv))))
+                push(dst, T.ip[:, a:b], T.rp[:, a:b], "arr%d" % c)
+    if cnt.get("sent", 0):
+        wait(g, "g", ("sent", cnt["sent"]))

@@ -3,29 +3,43 @@ from concourse.mybir import dt, AluOpType, ActivationFunctionType
 
 SIM_CORES = 112
 NC, G = 512, 4
-WIDTHS = (128, 128, 128, 128)
-K = len(WIDTHS)
-OFFS = tuple(sum(WIDTHS[:c]) for c in range(K))
+BW, K = 128, 4
+HW = NC // 2
+GROUPS = ((0,), (1,), (2,), (3, 4), (5,))
 CF = float(np.float32(0.0217))
+
+
+def _codes(n):
+    return ("sbuf", [128, n], "float8_e4m3fn_x4")
+
+
+def _plane(n):
+    return ("sbuf", [128, n], "uint8")
+
 
 SCRATCH = {
     "sb": ("sbuf", [128, 4 * NC], "bfloat16"),
     "xb": ("sbuf", [128, 4 * NC], "bfloat16"),
     "wb": ("sbuf", [128, 2 * G * 512], "bfloat16"),
     "vb": ("sbuf", [128, 512], "bfloat16"),
-    "sq": ("sbuf", [128, NC], "float8_e4m3fn_x4"), "sp": ("sbuf", [128, NC], "uint8"),
-    "xq": ("sbuf", [128, NC], "float8_e4m3fn_x4"), "xp": ("sbuf", [128, NC], "uint8"),
-    "wq": ("sbuf", [128, 2 * G * 128], "float8_e4m3fn_x4"), "wp": ("sbuf", [128, 2 * G * 128], "uint8"),
-    "vq": ("sbuf", [128, 128], "float8_e4m3fn_x4"), "vp": ("sbuf", [128, 128], "uint8"),
-    "iq": ("sbuf", [128, NC], "float8_e4m3fn_x4"), "ip": ("sbuf", [128, NC], "uint8"),
-    "hb": ("sbuf", [128, 4 * NC], "bfloat16"),
-    "hq": ("sbuf", [128, NC], "float8_e4m3fn_x4"), "hp": ("sbuf", [128, NC], "uint8"),
-    "rq": ("sbuf", [128, NC], "float8_e4m3fn_x4"), "rp": ("sbuf", [128, NC], "uint8"),
+    "sq": _codes(NC), "sp": _plane(NC),
+    "xq": _codes(NC), "xp": _plane(NC),
+    "wq": _codes(2 * G * 128), "wp": _plane(2 * G * 128),
+    "vq": _codes(128), "vp": _plane(128),
+    "w2q": _codes(2 * G * 128), "w2p": _plane(2 * G * 128),
+    "x2q": _codes(NC), "x2p": _plane(NC),
+    "iq": _codes(NC), "ip": _plane(NC),
+    "hbA": ("sbuf", [128, 4 * NC], "bfloat16"),
+    "hqA": _codes(NC), "hpA": _plane(NC),
+    "hbB": ("sbuf", [128, 4 * NC], "bfloat16"),
+    "hqB": _codes(NC), "hpB": _plane(NC),
+    "yq": _codes(NC), "yp": _plane(NC),
+    "rq": _codes(NC), "rp": _plane(NC),
     "yb": ("sbuf", [128, NC], "float32"),
     "ps": ("psum", [128, 8 * 512], "float32"),
 }
 SEMAPHORES = (["ls%d" % c for c in range(K)] + ["lx%d" % c for c in range(K)] + ["lw%d" % i for i in range(G)] + ["lv"]
-              + ["qz", "mm", "av", "ac", "hz", "yc", "yst", "sent"]
+              + ["qz", "mm", "av", "ac", "hz", "yc", "yst", "sent", "pin", "yin"]
               + ["arr%d" % c for c in range(K)] + ["relc%d" % c for c in range(K)] + ["relp%d" % c for c in range(K)])
 
 
@@ -33,26 +47,54 @@ def engines(m):
     return bin(m).count("1")
 
 
-def route(T, topo):
+def span(c):
+    return BW * c, BW * c + BW
+
+
+def plan(T, topo):
     cores = list(T.cores)
-    hops = []
-    for src, dst in zip(cores, cores[1:]):
+    line = [cores[gr[0]] for gr in GROUPS if len(gr) == 1]
+    feeder, tail = line[-2], line[-1]
+    pair = [cores[r] for gr in GROUPS if len(gr) == 2 for r in gr]
+    shippers = set(pair)
+
+    def way(src, dst):
+        return (1 if topo.may_write(src, dst) else 2, int(topo.chip(src) != topo.chip(dst)))
+
+    def cost(v):
+        legs = (way(feeder, v), way(v, tail))
+        return (sum(l[0] for l in legs), sum(l[1] for l in legs))
+
+    paths = sorted(pair, key=cost, reverse=True)
+
+    def relays(src, dst):
         if topo.may_write(src, dst):
-            hops.append((src, dst, None, None))
-            continue
+            return (None, None)
         cand = [c for c in range(SIM_CORES)
                 if c != src and c != dst and topo.chip(c) == topo.chip(src) and topo.may_write(c, dst)]
-        cand.sort(key=lambda c: (topo.die(c) != topo.die(src), c not in cores, c))
-        hops.append((src, dst, cand[0], cand[min(1, len(cand) - 1)]))
-    return hops
+
+        def shared(c):
+            return any(topo.chip(s) == topo.chip(c) and topo.die(s) == topo.die(c) for s in shippers)
+        cand.sort(key=lambda c: (c in shippers, shared(c), topo.die(c) != topo.die(src), c))
+        return (cand[0], cand[min(1, len(cand) - 1)])
+
+    hops = []
+    for src, dst in zip(line[:-2], line[1:-1]):
+        hops.append((src, dst, tuple(range(K))) + relays(src, dst))
+    for h, v in enumerate(paths):
+        hops.append((feeder, v, (2 * h, 2 * h + 1)) + relays(feeder, v))
+    for h, v in enumerate(paths):
+        hops.append((v, tail, (2 * h, 2 * h + 1)) + relays(v, tail))
+    return paths, hops
 
 
 def rank_program(g, core, T, topo):
-    hops = route(T, topo)
+    paths, hops = plan(T, topo)
     rank = T.rank_of(core)
-    if rank is None and not any(core in (h[2], h[3]) for h in hops):
+    if rank is None and not any(core in (h[3], h[4]) for h in hops):
         return
-    nranks = len(T.cores)
+    cores = list(T.cores)
+    nranks = len(cores)
     cnt, seen = {}, {}
 
     def mark(ins, name, n=1):
@@ -65,12 +107,47 @@ def rank_program(g, core, T, topo):
             seen[(qn, tok[0])] = tok[1]
             q.wait_ge(T.sem[tok[0]], tok[1])
 
-    hz = {}
+    def eng(a, b):
+        return engines(topo.mask(a, b))
+
+    def push(to, out_ap, in_ap, sem):
+        rid, pid = topo.addr(to)[:2]
+        m = topo.mask(core, to)
+        g.remote_dma(out_ap, in_ap, T.sem[sem], T.sem.sent, pid, rid, m)
+        cnt["sent"] = cnt.get("sent", 0) + engines(m)
+
+    def push_q(to, oq, op, iq_, ip_, a, b, sem):
+        push(to, oq[:, a:b].bitcast(dt.uint8), iq_[:, a:b].bitcast(dt.uint8), sem)
+        push(to, op[:, a:b], ip_[:, a:b], sem)
+
+    hz, qz = {}, {}
+    group, paired, partner, half = (), False, None, 0
+
+    def OUT(L):
+        return (T.hbA, T.hqA, T.hpA) if group.index(L) == 0 else (T.hbB, T.hqB, T.hpB)
+
     if rank is not None:
         PE, V, S, SY = g.tensor, g.vector, g.scalar, g.sync
         first, last = rank == 0, rank == nranks - 1
-        ld, qz, mm, act_t, yc_t = {}, {}, {}, {}, {}
+        group = [gr for gr in GROUPS if rank in gr][0]
+        paired = len(group) == 2
+        ld, mm, act_t, yc_t = {}, {}, {}, {}
         nld = [0]
+        if paired:
+            half = paths.index(core)
+            other_rank = group[0] + group[1] - rank
+            partner = cores[other_rank]
+            c0, c1 = 2 * half, 2 * half + 1
+            jobs = [(group[0], c0), (group[1], c0), (group[0], c1), (group[1], c1)]
+        elif not last:
+            jobs = [(rank, c) for c in range(K)]
+        else:
+            jobs = [(rank, c) for c in (0, 2, 1, 3)]
+        landed = {}
+        for src, dst, blks, cv, pv in hops:
+            if dst == core:
+                for c in blks:
+                    landed[c] = eng(src if cv is None else cv, dst) + eng(src if pv is None else pv, dst)
 
         def load(key, sem, buf, src, lo, hi):
             q = (SY, S)[nld[0] % 2]
@@ -81,86 +158,107 @@ def rank_program(g, core, T, topo):
             wait(V, "v", ld[key])
             qz[key] = mark(V.quantize_mx(codes[:, lo:hi], plane[:, lo:hi], buf[:, 4 * lo:4 * hi]), "qz")
 
-        def span(c):
-            return OFFS[c], OFFS[c] + WIDTHS[c]
-
-        def ld_s(c):
-            load(("s", c), "ls%d" % c, T.sb, T.s, 4 * span(c)[0], 4 * span(c)[1])
-
-        def ld_x(c):
-            load(("x", c), "lx%d" % c, T.xb, T.x, 4 * span(c)[0], 4 * span(c)[1])
-
-        def bank(c, i):
-            lo = 512 * (G * (c % 2) + i)
-            return T.ps[:, lo:lo + WIDTHS[c]]
+        def bank(j, i):
+            lo = 512 * (G * (j % 2) + i)
+            return T.ps[:, lo:lo + BW]
 
         if first:
             xkey, wkey = (lambda c: ("x", c)), (lambda i: ("w", i))
-            ld_s(0)
-            ld_x(0)
+            load(("s", 0), "ls0", T.sb, T.s, 0, 4 * BW)
+            load(("x", 0), "lx0", T.xb, T.x, 0, 4 * BW)
             for i in range(G):
                 load(("w", i), "lw%d" % i, T.wb, T.w, 1024 * i, 1024 * i + 1024)
             for c in range(1, K):
-                ld_s(c)
-                ld_x(c)
+                load(("s", c), "ls%d" % c, T.sb, T.s, 4 * span(c)[0], 4 * span(c)[1])
+                load(("x", c), "lx%d" % c, T.xb, T.x, 4 * span(c)[0], 4 * span(c)[1])
             load("v", "lv", T.vb, T.v, 0, 512)
-            iq, ip = T.sq, T.sp
         else:
-            xkey, wkey = (lambda c: ("x", 0)), (lambda i: ("w", i // 2))
+            wkey = lambda i: ("w", i // 2)
             for h in range(2):
                 load(("w", h), "lw%d" % h, T.wb, T.w, 2048 * h, 2048 * h + 2048)
-            load(("x", 0), "lx0", T.xb, T.x, 0, 4 * NC)
+            if paired:
+                xkey = lambda c: ("x", c // 2)
+                xs = (1 - half, half)
+                for h in xs:
+                    load(("x", h), "lx%d" % h, T.xb, T.x, 4 * HW * h, 4 * HW * h + 4 * HW)
+            else:
+                xkey = lambda c: ("x", 0)
+                load(("x", 0), "lx0", T.xb, T.x, 0, 4 * NC)
             load("v", "lv", T.vb, T.v, 0, 512)
             for h in range(2):
                 quant(("w", h), T.wq, T.wp, T.wb, 512 * h, 512 * h + 512)
-            quant(("x", 0), T.xq, T.xp, T.xb, 0, NC)
+            if paired:
+                for h in xs:
+                    quant(("x", h), T.xq, T.xp, T.xb, HW * h, HW * h + HW)
+            else:
+                quant(("x", 0), T.xq, T.xp, T.xb, 0, NC)
             quant("v", T.vq, T.vp, T.vb, 0, 128)
-            iq, ip = T.iq, T.ip
-            src, dst, cv, pv = hops[rank - 1]
-            landed = engines(topo.mask(src if cv is None else cv, dst)) + engines(topo.mask(src if pv is None else pv, dst))
 
-        def mm_x(c, i):
+        def sides(L, i, c):
+            if L == rank:
+                return T.wq, T.wp, T.xq, T.xp, [qz[wkey(i)], qz[xkey(c)]]
+            return T.w2q, T.w2p, T.x2q, T.x2p, [("pin", 6 * eng(partner, core))]
+
+        def mm_x(j, i):
+            L, c = jobs[j]
             a, b = span(c)
             k = 128 * (2 * i + 1)
-            wait(PE, "pe", qz[wkey(i)])
-            wait(PE, "pe", qz[xkey(c)])
-            if c >= 2:
-                wait(PE, "pe", act_t[(c - 2, i)])
-                if (c - 2, i) in yc_t:
-                    wait(PE, "pe", yc_t[(c - 2, i)])
-            PE.matmul_mx(bank(c, i), T.wq[:, k:k + 128], T.wp[:, k:k + 128], T.xq[:, a:b], T.xp[:, a:b], True, False)
+            wq, wp, xq, xp, toks = sides(L, i, c)
+            for t in toks:
+                wait(PE, "pe", t)
+            if j >= 2:
+                wait(PE, "pe", act_t[(j - 2, i)])
+                if (j - 2, i) in yc_t:
+                    wait(PE, "pe", yc_t[(j - 2, i)])
+            PE.matmul_mx(bank(j, i), wq[:, k:k + 128], wp[:, k:k + 128], xq[:, a:b], xp[:, a:b], True, False)
 
-        def mm_q(c, i):
+        def mm_q(j, i):
+            L, c = jobs[j]
             a, b = span(c)
             k = 128 * (2 * i)
+            wq, wp = sides(L, i, c)[:2]
             if first:
+                iq, ip = T.sq, T.sp
                 wait(PE, "pe", qz[("s", c)])
+            elif L == group[0]:
+                iq, ip = T.iq, T.ip
+                wait(PE, "pe", ("arr%d" % c, landed[c]))
             else:
-                wait(PE, "pe", ("arr%d" % c, landed))
-            mm[(c, i)] = mark(PE.matmul_mx(bank(c, i), T.wq[:, k:k + 128], T.wp[:, k:k + 128],
+                iq, ip = T.hqA, T.hpA
+                wait(PE, "pe", hz[(group[0], c)])
+            mm[(j, i)] = mark(PE.matmul_mx(bank(j, i), wq[:, k:k + 128], wp[:, k:k + 128],
                                            iq[:, a:b], ip[:, a:b], False, True), "mm")
 
-        def act(c, i, on_vector):
+        def act(j, i, on_vector):
+            L, c = jobs[j]
             a, b = span(c)
-            out = T.hb[:, 4 * a + i:4 * b:4]
+            out = OUT(L)[0][:, 4 * a + i:4 * b:4]
             if on_vector:
-                wait(V, "v", mm[(c, i)])
-                act_t[(c, i)] = mark(V.tensor_scalar(out, bank(c, i), 0.0, CF, AluOpType.max, AluOpType.mult), "av")
+                wait(V, "v", mm[(j, i)])
+                act_t[(j, i)] = mark(V.tensor_scalar(out, bank(j, i), 0.0, CF, AluOpType.max, AluOpType.mult), "av")
             else:
-                wait(S, "s", mm[(c, i)])
-                act_t[(c, i)] = mark(S.activation(out, bank(c, i), ActivationFunctionType.Relu, scale=CF), "ac")
+                wait(S, "s", mm[(j, i)])
+                act_t[(j, i)] = mark(S.activation(out, bank(j, i), ActivationFunctionType.Relu, scale=CF), "ac")
 
-        def pack(c):
+        def pack(j):
+            L, c = jobs[j]
             a, b = span(c)
+            hb, hq, hp = OUT(L)
             for i in range(G):
-                wait(V, "v", act_t[(c, i)])
-            hz[c] = mark(V.quantize_mx(T.hq[:, a:b], T.hp[:, a:b], T.hb[:, 4 * a:4 * b]), "hz")
+                wait(V, "v", act_t[(j, i)])
+            hz[(L, c)] = mark(V.quantize_mx(hq[:, a:b], hp[:, a:b], hb[:, 4 * a:4 * b]), "hz")
 
-        def y_part(a, b, out, users):
+        def run(j):
+            for i in range(G):
+                mm_q(j, i)
+                act(j, i, i % 2 == 0)
+            pack(j)
+
+        def y_part(cq, cp, a, b, out, users):
             wait(PE, "pe", qz["v"])
             for u in users:
                 wait(PE, "pe", u)
-            t = mark(PE.matmul_mx(out, T.vq[:], T.vp[:], T.hq[:, a:b], T.hp[:, a:b], True, True), "mm")
+            t = mark(PE.matmul_mx(out, T.vq[:], T.vp[:], cq[:, a:b], cp[:, a:b], True, True), "mm")
             wait(S, "s", t)
             t = mark(S.activation(T.yb[:, a:b], out, ActivationFunctionType.Copy), "yc")
             wait(SY, "sy", t)
@@ -188,54 +286,82 @@ def rank_program(g, core, T, topo):
                         mm_q(c, i)
                         act(c, i, False)
             quant("v", T.vq, T.vp, T.vb, 0, 128)
+            y_part(T.hqA, T.hpA, 0, NC, T.ps[:, 0:NC], [hz[(rank, K - 1)], act_t[(2, 0)]])
+        elif paired:
+            ahead = 2
+            for j in range(2):
+                for i in range(G):
+                    mm_x(j, i)
+            run(0)
+            run(1)
+            for i in range(G):
+                mm_x(2, i)
+            for i in range(ahead):
+                mm_x(3, i)
+            run(2)
+            for i in range(ahead, G):
+                mm_x(3, i)
+            run(3)
+            hq, hp = OUT(rank)[1:]
+            y_part(hq, hp, HW * half, HW * half + HW, T.ps[:, 0:HW], [hz[(rank, c1)], act_t[(2, 0)]])
+            o = HW * (1 - half)
+            y_part(T.yq, T.yp, o, o + HW, T.ps[:, 512:512 + HW], [("yin", 2 * eng(partner, core)), act_t[(2, 1)]])
         else:
-            for c in range(min(2, K)):
+            for j in range(2):
                 for i in range(G):
-                    mm_x(c, i)
+                    mm_x(j, i)
             later = []
-            for c in range(K):
+            for j in range(K):
                 for i in range(G):
-                    mm_q(c, i)
-                    act(c, i, i % 2 == 0)
-                for cc, ii in later:
-                    mm_x(cc, ii)
+                    mm_q(j, i)
+                    act(j, i, i % 2 == 0)
+                for jj, ii in later:
+                    mm_x(jj, ii)
                 later = []
-                pack(c)
-                if c + 2 < K:
+                pack(j)
+                if j + 2 < K:
                     for i in range(G):
                         if last and i == 0:
-                            later.append((c + 2, i))
+                            later.append((j + 2, i))
                         else:
-                            mm_x(c + 2, i)
+                            mm_x(j + 2, i)
+                c = jobs[j][1]
                 if last:
-                    yc_t[(c, 0)] = y_part(span(c)[0], span(c)[1], bank(c, 0), [hz[c], act_t[(c, 0)]])
-        if not last:
-            busy = [act_t[(c, 0)] for c in range(K) if c % 2 == 0]
-            y_part(0, NC, T.ps[:, 0:NC], [hz[K - 1], busy[-1]])
+                    yc_t[(j, 0)] = y_part(T.hqA, T.hpA, span(c)[0], span(c)[1], bank(j, 0), [hz[(rank, c)], act_t[(j, 0)]])
+            if not last:
+                y_part(T.hqA, T.hpA, 0, NC, T.ps[:, 0:NC], [hz[(rank, K - 1)], act_t[(2, 0)]])
         wait(SY, "sy", ("yst", cnt["yst"]))
 
-    def push(to, out_ap, in_ap, sem):
-        rid, pid = topo.addr(to)[:2]
-        m = topo.mask(core, to)
-        g.remote_dma(out_ap, in_ap, T.sem[sem], T.sem.sent, pid, rid, m)
-        cnt["sent"] = cnt.get("sent", 0) + engines(m)
+    if paired:
+        for h in range(2):
+            wait(g, "g", qz[("w", h)])
+            push_q(partner, T.w2q, T.w2p, T.wq, T.wp, 512 * h, 512 * h + 512, "pin")
+        o = HW * (1 - half)
+        wait(g, "g", qz[("x", 1 - half)])
+        push_q(partner, T.x2q, T.x2p, T.xq, T.xp, o, o + HW, "pin")
 
-    for src, dst, cv, pv in hops:
-        for c in range(K):
-            a, b = OFFS[c], OFFS[c] + WIDTHS[c]
+    for src, dst, blks, cv, pv in hops:
+        for c in blks:
+            a, b = span(c)
             if core == src:
-                wait(g, "g", hz[c])
+                hq, hp = OUT(group[-1])[1:]
+                wait(g, "g", hz[(group[-1], c)])
                 if cv is None:
-                    push(dst, T.iq[:, a:b].bitcast(dt.uint8), T.hq[:, a:b].bitcast(dt.uint8), "arr%d" % c)
-                    push(dst, T.ip[:, a:b], T.hp[:, a:b], "arr%d" % c)
+                    push_q(dst, T.iq, T.ip, hq, hp, a, b, "arr%d" % c)
                 else:
-                    push(cv, T.rq[:, a:b].bitcast(dt.uint8), T.hq[:, a:b].bitcast(dt.uint8), "relc%d" % c)
-                    push(pv, T.rp[:, a:b], T.hp[:, a:b], "relp%d" % c)
+                    push(cv, T.rq[:, a:b].bitcast(dt.uint8), hq[:, a:b].bitcast(dt.uint8), "relc%d" % c)
+                    push(pv, T.rp[:, a:b], hp[:, a:b], "relp%d" % c)
             if core == cv:
-                wait(g, "g", ("relc%d" % c, engines(topo.mask(src, cv))))
+                wait(g, "g", ("relc%d" % c, eng(src, cv)))
                 push(dst, T.iq[:, a:b].bitcast(dt.uint8), T.rq[:, a:b].bitcast(dt.uint8), "arr%d" % c)
             if core == pv:
-                wait(g, "g", ("relp%d" % c, engines(topo.mask(src, pv))))
+                wait(g, "g", ("relp%d" % c, eng(src, pv)))
                 push(dst, T.ip[:, a:b], T.rp[:, a:b], "arr%d" % c)
+
+    if paired:
+        L = group[0] + group[1] - rank
+        hq, hp = OUT(L)[1:]
+        wait(g, "g", hz[(L, 2 * half + 1)])
+        push_q(partner, T.yq, T.yp, hq, hp, HW * half, HW * half + HW, "yin")
     if cnt.get("sent", 0):
         wait(g, "g", ("sent", cnt["sent"]))

@@ -5,7 +5,7 @@ SIM_CORES = 112
 NC, G = 512, 4
 BW, K = 128, 4
 HW = NC // 2
-GROUPS = ((0,), (1,), (2,), (3, 4), (5,))
+OUTER, INNER = (2, 5), (3, 4)
 CF = float(np.float32(0.0217))
 
 
@@ -40,6 +40,7 @@ SCRATCH = {
 }
 SEMAPHORES = (["ls%d" % c for c in range(K)] + ["lx%d" % c for c in range(K)] + ["lw%d" % i for i in range(G)] + ["lv"]
               + ["qz", "mm", "av", "ac", "hz", "yc", "yst", "sent", "pin", "yin"]
+              + ["yb%d" % c for c in range(K)]
               + ["arr%d" % c for c in range(K)] + ["relc%d" % c for c in range(K)] + ["relp%d" % c for c in range(K)])
 
 
@@ -53,19 +54,39 @@ def span(c):
 
 def plan(T, topo):
     cores = list(T.cores)
-    line = [cores[gr[0]] for gr in GROUPS if len(gr) == 1]
-    feeder, tail = line[-2], line[-1]
-    pair = [cores[r] for gr in GROUPS if len(gr) == 2 for r in gr]
-    shippers = set(pair)
+    nl = len(cores)
+    tail = cores[-1]
+    outer = [cores[r] for r in OUTER]
+    inner = [cores[r] for r in INNER]
+    feeder = cores[OUTER[0] - 1]
+    shippers = set(outer + inner)
 
-    def way(src, dst):
-        return (1 if topo.may_write(src, dst) else 2, int(topo.chip(src) != topo.chip(dst)))
+    def writes(src, dst):
+        return 0 if src == dst else (1 if topo.may_write(src, dst) else 2)
 
-    def cost(v):
-        legs = (way(feeder, v), way(v, tail))
-        return (sum(l[0] for l in legs), sum(l[1] for l in legs))
-
-    paths = sorted(pair, key=cost, reverse=True)
+    best = None
+    for a in outer:
+        for b in inner:
+            a2 = outer[0] + outer[1] - a
+            b2 = inner[0] + inner[1] - b
+            ways = [writes(feeder, p) + writes(p, q) + writes(q, r) + writes(r, tail)
+                    for p, q, r in ((a, b, a2), (a2, b2, a))]
+            key = (sum(ways), ways[1])
+            if best is None or key < best[0]:
+                best = (key, a, a2, b, b2)
+    a, a2, b, b2 = best[1:]
+    owner = {}
+    for c in range(K):
+        h = c // 2
+        for L in range(nl):
+            if L == OUTER[0]:
+                owner[(L, c)] = (a, a2)[h]
+            elif L == OUTER[1]:
+                owner[(L, c)] = (a2, a)[h]
+            elif L in INNER:
+                owner[(L, c)] = (b, b2)[h]
+            else:
+                owner[(L, c)] = cores[L]
 
     def relays(src, dst):
         if topo.may_write(src, dst):
@@ -79,17 +100,16 @@ def plan(T, topo):
         return (cand[0], cand[min(1, len(cand) - 1)])
 
     hops = []
-    for src, dst in zip(line[:-2], line[1:-1]):
-        hops.append((src, dst, tuple(range(K))) + relays(src, dst))
-    for h, v in enumerate(paths):
-        hops.append((feeder, v, (2 * h, 2 * h + 1)) + relays(feeder, v))
-    for h, v in enumerate(paths):
-        hops.append((v, tail, (2 * h, 2 * h + 1)) + relays(v, tail))
-    return paths, hops
+    for L in range(1, nl):
+        for c in range(K):
+            src, dst = owner[(L - 1, c)], owner[(L, c)]
+            if src != dst:
+                hops.append((src, dst, c) + relays(src, dst) + (L - 1,))
+    return owner, hops
 
 
 def rank_program(g, core, T, topo):
-    paths, hops = plan(T, topo)
+    owner, hops = plan(T, topo)
     rank = T.rank_of(core)
     if rank is None and not any(core in (h[3], h[4]) for h in hops):
         return
@@ -121,7 +141,7 @@ def rank_program(g, core, T, topo):
         push(to, op[:, a:b], ip_[:, a:b], sem)
 
     hz, qz = {}, {}
-    group, paired, partner, half = (), False, None, 0
+    group, paired, partner, own, fore, prank = (rank,), False, None, 0, 0, None
 
     def OUT(L):
         return (T.hbA, T.hqA, T.hpA) if group.index(L) == 0 else (T.hbB, T.hqB, T.hpB)
@@ -129,25 +149,27 @@ def rank_program(g, core, T, topo):
     if rank is not None:
         PE, V, S, SY = g.tensor, g.vector, g.scalar, g.sync
         first, last = rank == 0, rank == nranks - 1
-        group = [gr for gr in GROUPS if rank in gr][0]
-        paired = len(group) == 2
+        for gr in (OUTER, INNER):
+            if rank in gr:
+                group, paired = gr, True
         ld, mm, act_t, yc_t = {}, {}, {}, {}
         nld = [0]
         if paired:
-            half = paths.index(core)
-            other_rank = group[0] + group[1] - rank
-            partner = cores[other_rank]
-            c0, c1 = 2 * half, 2 * half + 1
-            jobs = [(group[0], c0), (group[1], c0), (group[0], c1), (group[1], c1)]
-        elif not last:
-            jobs = [(rank, c) for c in range(K)]
+            prank = group[0] + group[1] - rank
+            partner = cores[prank]
+            own = [c for c in range(K) if owner[(rank, c)] == core][0] // 2
+            fore = [c for c in range(K) if owner[(prank, c)] == core][0] // 2
+            mine = [(L, c) for L in group for c in range(K) if owner[(L, c)] == core]
+            if own == fore:
+                jobs = sorted(mine, key=lambda t: (t[1], t[0]))
+            else:
+                jobs = sorted(mine)
         else:
-            jobs = [(rank, c) for c in (0, 2, 1, 3)]
+            jobs = [(rank, c) for c in range(K)]
         landed = {}
-        for src, dst, blks, cv, pv in hops:
+        for src, dst, c, cv, pv, L in hops:
             if dst == core:
-                for c in blks:
-                    landed[c] = eng(src if cv is None else cv, dst) + eng(src if pv is None else pv, dst)
+                landed[c] = eng(src if cv is None else cv, dst) + eng(src if pv is None else pv, dst)
 
         def load(key, sem, buf, src, lo, hi):
             q = (SY, S)[nld[0] % 2]
@@ -178,7 +200,7 @@ def rank_program(g, core, T, topo):
                 load(("w", h), "lw%d" % h, T.wb, T.w, 2048 * h, 2048 * h + 2048)
             if paired:
                 xkey = lambda c: ("x", c // 2)
-                xs = (1 - half, half)
+                xs = (1 - own, own)
                 for h in xs:
                     load(("x", h), "lx%d" % h, T.xb, T.x, 4 * HW * h, 4 * HW * h + 4 * HW)
             else:
@@ -220,12 +242,12 @@ def rank_program(g, core, T, topo):
             if first:
                 iq, ip = T.sq, T.sp
                 wait(PE, "pe", qz[("s", c)])
-            elif L == group[0]:
+            elif owner[(L - 1, c)] == core:
+                iq, ip = OUT(L - 1)[1:]
+                wait(PE, "pe", hz[(L - 1, c)])
+            else:
                 iq, ip = T.iq, T.ip
                 wait(PE, "pe", ("arr%d" % c, landed[c]))
-            else:
-                iq, ip = T.hqA, T.hpA
-                wait(PE, "pe", hz[(group[0], c)])
             mm[(j, i)] = mark(PE.matmul_mx(bank(j, i), wq[:, k:k + 128], wp[:, k:k + 128],
                                            iq[:, a:b], ip[:, a:b], False, True), "mm")
 
@@ -287,7 +309,7 @@ def rank_program(g, core, T, topo):
                         act(c, i, False)
             quant("v", T.vq, T.vp, T.vb, 0, 128)
             y_part(T.hqA, T.hpA, 0, NC, T.ps[:, 0:NC], [hz[(rank, K - 1)], act_t[(2, 0)]])
-        elif paired:
+        elif paired and own == fore:
             ahead = 2
             for j in range(2):
                 for i in range(G):
@@ -303,65 +325,83 @@ def rank_program(g, core, T, topo):
                 mm_x(3, i)
             run(3)
             hq, hp = OUT(rank)[1:]
-            y_part(hq, hp, HW * half, HW * half + HW, T.ps[:, 0:HW], [hz[(rank, c1)], act_t[(2, 0)]])
-            o = HW * (1 - half)
+            y_part(hq, hp, HW * own, HW * own + HW, T.ps[:, 0:HW], [hz[(rank, 2 * own + 1)], act_t[(2, 0)]])
+            o = HW * (1 - own)
             y_part(T.yq, T.yp, o, o + HW, T.ps[:, 512:512 + HW], [("yin", 2 * eng(partner, core)), act_t[(2, 1)]])
+        elif paired:
+            for j in range(2):
+                for i in range(G):
+                    mm_x(j, i)
+            run(0)
+            run(1)
+            if not last:
+                hq, hp = OUT(rank)[1:]
+                yc_t[(0, 0)] = y_part(hq, hp, HW * own, HW * own + HW, T.ps[:, 0:HW],
+                                      [hz[(rank, 2 * own + 1)], act_t[(0, 0)]])
+                o = HW * (1 - own)
+                yc_t[(0, 1)] = y_part(T.yq, T.yp, o, o + HW, T.ps[:, 512:512 + HW],
+                                      [("yin", 2 * eng(partner, core)), act_t[(0, 1)]])
+            for j in range(2, K):
+                for i in range(G):
+                    mm_x(j, i)
+            if not last:
+                run(2)
+                run(3)
+            else:
+                hq, hp = OUT(rank)[1:]
+                theirs = [c for c in range(K) if owner[(rank, c)] != core]
+                for n, j in enumerate((2, 3)):
+                    run(j)
+                    c = jobs[j][1]
+                    y_part(hq, hp, span(c)[0], span(c)[1], bank(j, 0), [hz[(rank, c)], act_t[(j, 0)]])
+                    c = theirs[n]
+                    y_part(T.yq, T.yp, span(c)[0], span(c)[1], bank(2, 1 + n),
+                           [("yb%d" % c, 2 * eng(partner, core)), act_t[(2, 1 + n)]])
         else:
             for j in range(2):
                 for i in range(G):
                     mm_x(j, i)
-            later = []
             for j in range(K):
-                for i in range(G):
-                    mm_q(j, i)
-                    act(j, i, i % 2 == 0)
-                for jj, ii in later:
-                    mm_x(jj, ii)
-                later = []
-                pack(j)
+                run(j)
                 if j + 2 < K:
                     for i in range(G):
-                        if last and i == 0:
-                            later.append((j + 2, i))
-                        else:
-                            mm_x(j + 2, i)
-                c = jobs[j][1]
-                if last:
-                    yc_t[(j, 0)] = y_part(T.hqA, T.hpA, span(c)[0], span(c)[1], bank(j, 0), [hz[(rank, c)], act_t[(j, 0)]])
-            if not last:
-                y_part(T.hqA, T.hpA, 0, NC, T.ps[:, 0:NC], [hz[(rank, K - 1)], act_t[(2, 0)]])
+                        mm_x(j + 2, i)
+            y_part(T.hqA, T.hpA, 0, NC, T.ps[:, 0:NC], [hz[(rank, K - 1)], act_t[(2, 0)]])
         wait(SY, "sy", ("yst", cnt["yst"]))
 
     if paired:
         for h in range(2):
             wait(g, "g", qz[("w", h)])
             push_q(partner, T.w2q, T.w2p, T.wq, T.wp, 512 * h, 512 * h + 512, "pin")
-        o = HW * (1 - half)
-        wait(g, "g", qz[("x", 1 - half)])
+        o = HW * (1 - own)
+        wait(g, "g", qz[("x", 1 - own)])
         push_q(partner, T.x2q, T.x2p, T.xq, T.xp, o, o + HW, "pin")
 
-    for src, dst, blks, cv, pv in hops:
-        for c in blks:
-            a, b = span(c)
-            if core == src:
-                hq, hp = OUT(group[-1])[1:]
-                wait(g, "g", hz[(group[-1], c)])
-                if cv is None:
-                    push_q(dst, T.iq, T.ip, hq, hp, a, b, "arr%d" % c)
-                else:
-                    push(cv, T.rq[:, a:b].bitcast(dt.uint8), hq[:, a:b].bitcast(dt.uint8), "relc%d" % c)
-                    push(pv, T.rp[:, a:b], hp[:, a:b], "relp%d" % c)
-            if core == cv:
-                wait(g, "g", ("relc%d" % c, eng(src, cv)))
-                push(dst, T.iq[:, a:b].bitcast(dt.uint8), T.rq[:, a:b].bitcast(dt.uint8), "arr%d" % c)
-            if core == pv:
-                wait(g, "g", ("relp%d" % c, eng(src, pv)))
-                push(dst, T.ip[:, a:b], T.rp[:, a:b], "arr%d" % c)
+    for src, dst, c, cv, pv, L in hops:
+        a, b = span(c)
+        if core == src:
+            hq, hp = OUT(L)[1:]
+            wait(g, "g", hz[(L, c)])
+            if cv is None:
+                push_q(dst, T.iq, T.ip, hq, hp, a, b, "arr%d" % c)
+            else:
+                push(cv, T.rq[:, a:b].bitcast(dt.uint8), hq[:, a:b].bitcast(dt.uint8), "relc%d" % c)
+                push(pv, T.rp[:, a:b], hp[:, a:b], "relp%d" % c)
+        if core == cv:
+            wait(g, "g", ("relc%d" % c, eng(src, cv)))
+            push(dst, T.iq[:, a:b].bitcast(dt.uint8), T.rq[:, a:b].bitcast(dt.uint8), "arr%d" % c)
+        if core == pv:
+            wait(g, "g", ("relp%d" % c, eng(src, pv)))
+            push(dst, T.ip[:, a:b], T.rp[:, a:b], "arr%d" % c)
 
     if paired:
-        L = group[0] + group[1] - rank
-        hq, hp = OUT(L)[1:]
-        wait(g, "g", hz[(L, 2 * half + 1)])
-        push_q(partner, T.yq, T.yp, hq, hp, HW * half, HW * half + HW, "yin")
+        hq, hp = OUT(prank)[1:]
+        if prank == nranks - 1:
+            for c in (2 * fore, 2 * fore + 1):
+                wait(g, "g", hz[(prank, c)])
+                push_q(partner, T.yq, T.yp, hq, hp, span(c)[0], span(c)[1], "yb%d" % c)
+        else:
+            wait(g, "g", hz[(prank, 2 * fore + 1)])
+            push_q(partner, T.yq, T.yp, hq, hp, HW * fore, HW * fore + HW, "yin")
     if cnt.get("sent", 0):
         wait(g, "g", ("sent", cnt["sent"]))

@@ -35,11 +35,12 @@ SCRATCH = {
     "hqB": _codes(NC), "hpB": _plane(NC),
     "yq": _codes(NC), "yp": _plane(NC),
     "rq": _codes(NC), "rp": _plane(NC),
+    "tp": _plane(2 * G * 128),
     "yb": ("sbuf", [128, NC], "float32"),
     "ps": ("psum", [128, 8 * 512], "float32"),
 }
 SEMAPHORES = (["ls%d" % c for c in range(K)] + ["lx%d" % c for c in range(K)] + ["lw%d" % i for i in range(G)] + ["lv"]
-              + ["qz", "mm", "av", "ac", "hz", "yc", "yst", "sent", "pin", "yin"]
+              + ["qz", "mm", "av", "ac", "hz", "yc", "yst", "sent", "pin", "yin", "tin"]
               + ["yb%d" % c for c in range(K)]
               + ["arr%d" % c for c in range(K)] + ["relc%d" % c for c in range(K)] + ["relp%d" % c for c in range(K)])
 
@@ -108,10 +109,49 @@ def plan(T, topo):
     return owner, hops
 
 
+def byways(T, topo, hops):
+    cores = list(T.cores)
+    busy = set(cores[r] for r in OUTER + INNER)
+    free = []
+    for src, dst, c, cv, pv, L in hops:
+        for v in (src, cv, pv):
+            if v is not None and v not in busy and v not in free:
+                free.append(v)
+    chain = list(free)
+    half = G * 128
+    ways, cuts = {}, {}
+    for a, b in (INNER, INNER[::-1]):
+        s, d = cores[a], cores[b]
+        here = [v for v in free if topo.chip(v) == topo.chip(s)]
+        near = [v for v in here if topo.may_write(v, d)][:2]
+        head = [v for v in here if not topo.may_write(v, d)][:1]
+        on = [c for c in range(SIM_CORES) if topo.chip(c) == topo.chip(s) and topo.may_write(c, d)
+              and c not in busy and c not in chain]
+        if not on:
+            head = []
+        far = [v for v in free if topo.chip(v) == topo.chip(d) and topo.may_write(s, v)][:1]
+        free = [v for v in free if v not in near + head + far]
+        w, cut, lo = [], [0], 0
+        if head:
+            w.append((0, BW, (head[0], on[0])))
+            lo = BW
+            cut.append(BW)
+        if near:
+            step = (half - lo) // len(near)
+            w += [(lo + step * n, lo + step * n + step, (v,)) for n, v in enumerate(near)]
+        else:
+            w.append((lo, half, ()))
+        w.append((half, 2 * half, (far[0],) if far else ()))
+        ways[s], cuts[s] = w, cut + [half, 2 * half]
+    return ways, cuts
+
+
 def rank_program(g, core, T, topo):
     owner, hops = plan(T, topo)
+    ways, cuts = byways(T, topo, hops)
     rank = T.rank_of(core)
-    if rank is None and not any(core in (h[3], h[4]) for h in hops):
+    if (rank is None and not any(core in (h[3], h[4]) for h in hops)
+            and not any(core in p[2] for w in ways.values() for p in w)):
         return
     cores = list(T.cores)
     nranks = len(cores)
@@ -139,6 +179,12 @@ def rank_program(g, core, T, topo):
     def push_q(to, oq, op, iq_, ip_, a, b, sem):
         push(to, oq[:, a:b].bitcast(dt.uint8), iq_[:, a:b].bitcast(dt.uint8), sem)
         push(to, op[:, a:b], ip_[:, a:b], sem)
+
+    def pieces(s):
+        return ways.get(s, [(0, G * 128, ()), (G * 128, 2 * G * 128, ())])
+
+    def cutting(s):
+        return cuts.get(s, [0, G * 128, 2 * G * 128])
 
     hz, qz = {}, {}
     group, paired, partner, own, fore, prank = (rank,), False, None, 0, 0, None
@@ -195,9 +241,10 @@ def rank_program(g, core, T, topo):
                 load(("x", c), "lx%d" % c, T.xb, T.x, 4 * span(c)[0], 4 * span(c)[1])
             load("v", "lv", T.vb, T.v, 0, 512)
         else:
-            wkey = lambda i: ("w", i // 2)
-            for h in range(2):
-                load(("w", h), "lw%d" % h, T.wb, T.w, 2048 * h, 2048 * h + 2048)
+            cut = cutting(core)
+            wkey = lambda i: ("w", max(n for n in range(len(cut) - 1) if cut[n] < 256 * i + 256))
+            for n in range(len(cut) - 1):
+                load(("w", n), "lw%d" % n, T.wb, T.w, 4 * cut[n], 4 * cut[n + 1])
             if paired:
                 xkey = lambda c: ("x", c // 2)
                 xs = (1 - own, own)
@@ -207,8 +254,8 @@ def rank_program(g, core, T, topo):
                 xkey = lambda c: ("x", 0)
                 load(("x", 0), "lx0", T.xb, T.x, 0, 4 * NC)
             load("v", "lv", T.vb, T.v, 0, 512)
-            for h in range(2):
-                quant(("w", h), T.wq, T.wp, T.wb, 512 * h, 512 * h + 512)
+            for n in range(len(cut) - 1):
+                quant(("w", n), T.wq, T.wp, T.wb, cut[n], cut[n + 1])
             if paired:
                 for h in xs:
                     quant(("x", h), T.xq, T.xp, T.xb, HW * h, HW * h + HW)
@@ -219,7 +266,8 @@ def rank_program(g, core, T, topo):
         def sides(L, i, c):
             if L == rank:
                 return T.wq, T.wp, T.xq, T.xp, [qz[wkey(i)], qz[xkey(c)]]
-            return T.w2q, T.w2p, T.x2q, T.x2p, [("pin", 6 * eng(partner, core))]
+            return T.w2q, T.w2p, T.x2q, T.x2p, [("pin", (len(cutting(partner)) + 1) * eng(partner, core) + sum(
+                eng(p[-1] if p else partner, core) for lo, hi, p in pieces(partner)))]
 
         def mm_x(j, i):
             L, c = jobs[j]
@@ -370,12 +418,30 @@ def rank_program(g, core, T, topo):
         wait(SY, "sy", ("yst", cnt["yst"]))
 
     if paired:
-        for h in range(2):
-            wait(g, "g", qz[("w", h)])
-            push_q(partner, T.w2q, T.w2p, T.wq, T.wp, 512 * h, 512 * h + 512, "pin")
+        cut = cutting(core)
+        for n in range(len(cut) - 1):
+            wait(g, "g", qz[("w", n)])
+            part = [p for p in pieces(core) if cut[n] <= p[0] < cut[n + 1]]
+            for lo, hi, p in part:
+                if p:
+                    push(p[0], T.tp[:, lo:hi], T.wp[:, lo:hi], "tin")
+            push(partner, T.w2q[:, cut[n]:cut[n + 1]].bitcast(dt.uint8), T.wq[:, cut[n]:cut[n + 1]].bitcast(dt.uint8), "pin")
+            for lo, hi, p in part:
+                if not p:
+                    push(partner, T.w2p[:, lo:hi], T.wp[:, lo:hi], "pin")
         o = HW * (1 - own)
         wait(g, "g", qz[("x", 1 - own)])
         push_q(partner, T.x2q, T.x2p, T.xq, T.xp, o, o + HW, "pin")
+
+    for s in ways:
+        for lo, hi, p in ways[s]:
+            if core in p:
+                k = p.index(core)
+                wait(g, "g", ("tin", eng(s if k == 0 else p[k - 1], core)))
+                if k + 1 < len(p):
+                    push(p[k + 1], T.tp[:, lo:hi], T.tp[:, lo:hi], "tin")
+                else:
+                    push([cores[r] for r in INNER if cores[r] != s][0], T.w2p[:, lo:hi], T.tp[:, lo:hi], "pin")
 
     for src, dst, c, cv, pv, L in hops:
         a, b = span(c)

import numpy as np
from concourse.mybir import dt, AluOpType, ActivationFunctionType

SIM_CORES = 112
NC, G = 512, 4
BW, K = 128, 4
HW = NC // 2
OUTER, INNER = (2, 5), (3, 4)
CF = float(np.float32(0.0217))


def _codes(n):
    return ("sbuf", [128, n], "float8_e4m3fn_x4")


def _plane(n):
    return ("sbuf", [128, n], "uint8")


SCRATCH = {
    "sb": ("sbuf", [128, 4 * NC], "bfloat16"),
    "xb": ("sbuf", [128, 4 * NC], "bfloat16"),
    "wb": ("sbuf", [128, 2 * G * 512], "bfloat16"),
    "vb": ("sbuf", [128, 512], "bfloat16"),
    "sq": _codes(NC), "sp": _plane(NC),
    "xq": _codes(NC), "xp": _plane(NC),
    "wq": _codes(2 * G * 128), "wp": _plane(2 * G * 128),
    "vq": _codes(128), "vp": _plane(128),
    "w2q": _codes(2 * G * 128), "w2p": _plane(2 * G * 128),
    "x2q": _codes(NC), "x2p": _plane(NC),
    "iq": _codes(NC), "ip": _plane(NC),
    "hbA": ("sbuf", [128, 4 * NC], "bfloat16"),
    "hqA": _codes(NC), "hpA": _plane(NC),
    "hbB": ("sbuf", [128, 4 * NC], "bfloat16"),
    "hqB": _codes(NC), "hpB": _plane(NC),
    "yq": _codes(NC), "yp": _plane(NC),
    "rq": _codes(NC), "rp": _plane(NC),
    "tp": _plane(2 * G * 128),
    "yb": ("sbuf", [128, NC], "float32"),
    "ps": ("psum", [128, 8 * 512], "float32"),
}
SEMAPHORES = (["ls%d" % c for c in range(K)] + ["lx%d" % c for c in range(K)] + ["lw%d" % i for i in range(G)] + ["lv"]
              + ["qz", "mm", "av", "ac", "hz", "yc", "yst", "sent", "pin", "yin", "tin"]
              + ["yb%d" % c for c in range(K)]
              + ["arr%d" % c for c in range(K)] + ["relc%d" % c for c in range(K)] + ["relp%d" % c for c in range(K)])


def engines(m):
    return bin(m).count("1")


def span(c):
    return BW * c, BW * c + BW


def plan(T, topo):
    cores = list(T.cores)
    nl = len(cores)
    tail = cores[-1]
    outer = [cores[r] for r in OUTER]
    inner = [cores[r] for r in INNER]
    feeder = cores[OUTER[0] - 1]
    shippers = set(outer + inner)

    def writes(src, dst):
        return 0 if src == dst else (1 if topo.may_write(src, dst) else 2)

    best = None
    for a in outer:
        for b in inner:
            a2 = outer[0] + outer[1] - a
            b2 = inner[0] + inner[1] - b
            ways = [writes(feeder, p) + writes(p, q) + writes(q, r) + writes(r, tail)
                    for p, q, r in ((a, b, a2), (a2, b2, a))]
            key = (sum(ways), ways[1])
            if best is None or key < best[0]:
                best = (key, a, a2, b, b2)
    a, a2, b, b2 = best[1:]
    owner = {}
    for c in range(K):
        h = c // 2
        for L in range(nl):
            if L == OUTER[0]:
                owner[(L, c)] = (a, a2)[h]
            elif L == OUTER[1]:
                owner[(L, c)] = (a2, a)[h]
            elif L in INNER:
                owner[(L, c)] = (b, b2)[h]
            else:
                owner[(L, c)] = cores[L]

    def relays(src, dst):
        if topo.may_write(src, dst):
            return (None, None)
        cand = [c for c in range(SIM_CORES)
                if c != src and c != dst and topo.chip(c) == topo.chip(src) and topo.may_write(c, dst)]

        def shared(c):
            return any(topo.chip(s) == topo.chip(c) and topo.die(s) == topo.die(c) for s in shippers)
        cand.sort(key=lambda c: (c in shippers, shared(c), topo.die(c) != topo.die(src), c))
        return (cand[0], cand[min(1, len(cand) - 1)])

    hops = []
    for L in range(1, nl):
        for c in range(K):
            src, dst = owner[(L - 1, c)], owner[(L, c)]
            if src != dst:
                hops.append((src, dst, c) + relays(src, dst) + (L - 1,))
    return owner, hops


def byways(T, topo, hops):
    cores = list(T.cores)
    busy = set(cores[r] for r in OUTER + INNER)
    free = []
    for src, dst, c, cv, pv, L in hops:
        for v in (src, cv, pv):
            if v is not None and v not in busy and v not in free:
                free.append(v)
    chain = list(free)
    half = G * 128
    ways, cuts = {}, {}
    for a, b in (INNER, INNER[::-1]):
        s, d = cores[a], cores[b]
        here = [v for v in free if topo.chip(v) == topo.chip(s)]
        near = [v for v in here if topo.may_write(v, d)][:2]
        head = [v for v in here if not topo.may_write(v, d)][:1]
        on = [c for c in range(SIM_CORES) if topo.chip(c) == topo.chip(s) and topo.may_write(c, d)
              and c not in busy and c not in chain]
        if not on:
            head = []
        far = [v for v in free if topo.chip(v) == topo.chip(d) and topo.may_write(s, v)][:1]
        free = [v for v in free if v not in near + head + far]
        w, cut, lo = [], [0], 0
        if head:
            w.append((0, BW, (head[0], on[0])))
            lo = BW
            cut.append(BW)
        if near:
            step = (half - lo) // len(near)
            w += [(lo + step * n, lo + step * n + step, (v,)) for n, v in enumerate(near)]
        else:
            w.append((lo, half, ()))
        w.append((half, 2 * half, (far[0],) if far else ()))
        ways[s], cuts[s] = w, cut + [half, 2 * half]
    return ways, cuts


def rank_program(g, core, T, topo):
    owner, hops = plan(T, topo)
    ways, cuts = byways(T, topo, hops)
    rank = T.rank_of(core)
    if (rank is None and not any(core in (h[3], h[4]) for h in hops)
            and not any(core in p[2] for w in ways.values() for p in w)):
        return
    cores = list(T.cores)
    nranks = len(cores)
    cnt, seen = {}, {}

    def mark(ins, name, n=1):
        cnt[name] = cnt.get(name, 0) + n
        ins.then_inc(T.sem[name], n)
        return (name, cnt[name])

    def wait(q, qn, tok):
        if seen.get((qn, tok[0]), 0) < tok[1]:
            seen[(qn, tok[0])] = tok[1]
            q.wait_ge(T.sem[tok[0]], tok[1])

    def eng(a, b):
        return engines(topo.mask(a, b))

    def push(to, out_ap, in_ap, sem):
        rid, pid = topo.addr(to)[:2]
        m = topo.mask(core, to)
        g.remote_dma(out_ap, in_ap, T.sem[sem], T.sem.sent, pid, rid, m)
        cnt["sent"] = cnt.get("sent", 0) + engines(m)

    def push_q(to, oq, op, iq_, ip_, a, b, sem):
        push(to, oq[:, a:b].bitcast(dt.uint8), iq_[:, a:b].bitcast(dt.uint8), sem)
        push(to, op[:, a:b], ip_[:, a:b], sem)

    def pieces(s):
        return ways.get(s, [(0, G * 128, ()), (G * 128, 2 * G * 128, ())])

    def cutting(s):
        return cuts.get(s, [0, G * 128, 2 * G * 128])

    hz, qz = {}, {}
    group, paired, partner, own, fore, prank = (rank,), False, None, 0, 0, None

    def OUT(L):
        return (T.hbA, T.hqA, T.hpA) if group.index(L) == 0 else (T.hbB, T.hqB, T.hpB)

    if rank is not None:
        PE, V, S, SY = g.tensor, g.vector, g.scalar, g.sync
        first, last = rank == 0, rank == nranks - 1
        for gr in (OUTER, INNER):
            if rank in gr:
                group, paired = gr, True
        ld, mm, act_t, yc_t = {}, {}, {}, {}
        nld = [0]
        if paired:
            prank = group[0] + group[1] - rank
            partner = cores[prank]
            own = [c for c in range(K) if owner[(rank, c)] == core][0] // 2
            fore = [c for c in range(K) if owner[(prank, c)] == core][0] // 2
            mine = [(L, c) for L in group for c in range(K) if owner[(L, c)] == core]
            if own == fore:
                jobs = sorted(mine, key=lambda t: (t[1], t[0]))
            else:
                jobs = sorted(mine)
        else:
            jobs = [(rank, c) for c in range(K)]
        landed = {}
        for src, dst, c, cv, pv, L in hops:
            if dst == core:
                landed[c] = eng(src if cv is None else cv, dst) + eng(src if pv is None else pv, dst)

        def load(key, sem, buf, src, lo, hi):
            q = (SY, S)[nld[0] % 2]
            nld[0] += 1
            ld[key] = mark(q.dma_start(buf[:, lo:hi], src[:, lo:hi]), sem, 16)

        def quant(key, codes, plane, buf, lo, hi):
            wait(V, "v", ld[key])
            qz[key] = mark(V.quantize_mx(codes[:, lo:hi], plane[:, lo:hi], buf[:, 4 * lo:4 * hi]), "qz")

        def bank(j, i):
            lo = 512 * (G * (j % 2) + i)
            return T.ps[:, lo:lo + BW]

        if first:
            xkey, wkey = (lambda c: ("x", c)), (lambda i: ("w", i))
            load(("s", 0), "ls0", T.sb, T.s, 0, 4 * BW)
            load(("x", 0), "lx0", T.xb, T.x, 0, 4 * BW)
            for i in range(G):
                load(("w", i), "lw%d" % i, T.wb, T.w, 1024 * i, 1024 * i + 1024)
            for c in range(1, K):
                load(("s", c), "ls%d" % c, T.sb, T.s, 4 * span(c)[0], 4 * span(c)[1])
                load(("x", c), "lx%d" % c, T.xb, T.x, 4 * span(c)[0], 4 * span(c)[1])
            load("v", "lv", T.vb, T.v, 0, 512)
        else:
            cut = cutting(core)
            wkey = lambda i: ("w", max(n for n in range(len(cut) - 1) if cut[n] < 256 * i + 256))
            for n in range(len(cut) - 1):
                load(("w", n), "lw%d" % n, T.wb, T.w, 4 * cut[n], 4 * cut[n + 1])
            if paired:
                xkey = lambda c: ("x", c // 2)
                xs = (1 - own, own)
                for h in xs:
                    load(("x", h), "lx%d" % h, T.xb, T.x, 4 * HW * h, 4 * HW * h + 4 * HW)
            else:
                xkey = lambda c: ("x", 0)
                load(("x", 0), "lx0", T.xb, T.x, 0, 4 * NC)
            load("v", "lv", T.vb, T.v, 0, 512)
            for n in range(len(cut) - 1):
                quant(("w", n), T.wq, T.wp, T.wb, cut[n], cut[n + 1])
            if paired:
                for h in xs:
                    quant(("x", h), T.xq, T.xp, T.xb, HW * h, HW * h + HW)
            else:
                quant(("x", 0), T.xq, T.xp, T.xb, 0, NC)
            quant("v", T.vq, T.vp, T.vb, 0, 128)

        def sides(L, i, c):
            if L == rank:
                return T.wq, T.wp, T.xq, T.xp, [qz[wkey(i)], qz[xkey(c)]]
            return T.w2q, T.w2p, T.x2q, T.x2p, [("pin", (len(cutting(partner)) + 1) * eng(partner, core) + sum(
                eng(p[-1] if p else partner, core) for lo, hi, p in pieces(partner)))]

        def mm_x(j, i):
            L, c = jobs[j]
            a, b = span(c)
            k = 128 * (2 * i + 1)
            wq, wp, xq, xp, toks = sides(L, i, c)
            for t in toks:
                wait(PE, "pe", t)
            if j >= 2:
                wait(PE, "pe", act_t[(j - 2, i)])
                if (j - 2, i) in yc_t:
                    wait(PE, "pe", yc_t[(j - 2, i)])
            PE.matmul_mx(bank(j, i), wq[:, k:k + 128], wp[:, k:k + 128], xq[:, a:b], xp[:, a:b], True, False)

        def mm_q(j, i):
            L, c = jobs[j]
            a, b = span(c)
            k = 128 * (2 * i)
            wq, wp = sides(L, i, c)[:2]
            if first:
                iq, ip = T.sq, T.sp
                wait(PE, "pe", qz[("s", c)])
            elif owner[(L - 1, c)] == core:
                iq, ip = OUT(L - 1)[1:]
                wait(PE, "pe", hz[(L - 1, c)])
            else:
                iq, ip = T.iq, T.ip
                wait(PE, "pe", ("arr%d" % c, landed[c]))
            mm[(j, i)] = mark(PE.matmul_mx(bank(j, i), wq[:, k:k + 128], wp[:, k:k + 128],
                                           iq[:, a:b], ip[:, a:b], False, True), "mm")

        def act(j, i, on_vector):
            L, c = jobs[j]
            a, b = span(c)
            out = OUT(L)[0][:, 4 * a + i:4 * b:4]
            if on_vector:
                wait(V, "v", mm[(j, i)])
                act_t[(j, i)] = mark(V.tensor_scalar(out, bank(j, i), 0.0, CF, AluOpType.max, AluOpType.mult), "av")
            else:
                wait(S, "s", mm[(j, i)])
                act_t[(j, i)] = mark(S.activation(out, bank(j, i), ActivationFunctionType.Relu, scale=CF), "ac")

        def pack(j):
            L, c = jobs[j]
            a, b = span(c)
            hb, hq, hp = OUT(L)
            for i in range(G):
                wait(V, "v", act_t[(j, i)])
            hz[(L, c)] = mark(V.quantize_mx(hq[:, a:b], hp[:, a:b], hb[:, 4 * a:4 * b]), "hz")

        def run(j):
            for i in range(G):
                mm_q(j, i)
                act(j, i, i % 2 == 0)
            pack(j)

        def y_part(cq, cp, a, b, out, users):
            wait(PE, "pe", qz["v"])
            for u in users:
                wait(PE, "pe", u)
            t = mark(PE.matmul_mx(out, T.vq[:], T.vp[:], cq[:, a:b], cp[:, a:b], True, True), "mm")
            wait(S, "s", t)
            t = mark(S.activation(T.yb[:, a:b], out, ActivationFunctionType.Copy), "yc")
            wait(SY, "sy", t)
            mark(SY.dma_start(T.y[:, a:b], T.yb[:, a:b]), "yst", 16)
            return t

        if first:
            quant(("s", 0), T.sq, T.sp, T.sb, *span(0))
            quant(("x", 0), T.xq, T.xp, T.xb, *span(0))
            for i in range(G):
                quant(("w", i), T.wq, T.wp, T.wb, 256 * i, 256 * i + 256)
                mm_x(0, i)
                mm_q(0, i)
                act(0, i, False)
            pack(0)
            for c in range(1, K + 1):
                if c < K:
                    quant(("s", c), T.sq, T.sp, T.sb, *span(c))
                    quant(("x", c), T.xq, T.xp, T.xb, *span(c))
                if c >= 2:
                    pack(c - 1)
                if c < K:
                    for i in range(G):
                        mm_x(c, i)
                        mm_q(c, i)
                        act(c, i, False)
            quant("v", T.vq, T.vp, T.vb, 0, 128)
            y_part(T.hqA, T.hpA, 0, NC, T.ps[:, 0:NC], [hz[(rank, K - 1)], act_t[(2, 0)]])
        elif paired and own == fore:
            ahead = 2
            for j in range(2):
                for i in range(G):
                    mm_x(j, i)
            run(0)
            run(1)
            for i in range(G):
                mm_x(2, i)
            for i in range(ahead):
                mm_x(3, i)
            run(2)
            for i in range(ahead, G):
                mm_x(3, i)
            run(3)
            hq, hp = OUT(rank)[1:]
            y_part(hq, hp, HW * own, HW * own + HW, T.ps[:, 0:HW], [hz[(rank, 2 * own + 1)], act_t[(2, 0)]])
            o = HW * (1 - own)
            y_part(T.yq, T.yp, o, o + HW, T.ps[:, 512:512 + HW], [("yin", 2 * eng(partner, core)), act_t[(2, 1)]])
        elif paired:
            for j in range(2):
                for i in range(G):
                    mm_x(j, i)
            run(0)
            run(1)
            if not last:
                hq, hp = OUT(rank)[1:]
                yc_t[(0, 0)] = y_part(hq, hp, HW * own, HW * own + HW, T.ps[:, 0:HW],
                                      [hz[(rank, 2 * own + 1)], act_t[(0, 0)]])
                o = HW * (1 - own)
                yc_t[(0, 1)] = y_part(T.yq, T.yp, o, o + HW, T.ps[:, 512:512 + HW],
                                      [("yin", 2 * eng(partner, core)), act_t[(0, 1)]])
            for j in range(2, K):
                for i in range(G):
                    mm_x(j, i)
            if not last:
                run(2)
                run(3)
            else:
                hq, hp = OUT(rank)[1:]
                theirs = [c for c in range(K) if owner[(rank, c)] != core]
                for n, j in enumerate((2, 3)):
                    run(j)
                    c = jobs[j][1]
                    y_part(hq, hp, span(c)[0], span(c)[1], bank(j, 0), [hz[(rank, c)], act_t[(j, 0)]])
                    c = theirs[n]
                    y_part(T.yq, T.yp, span(c)[0], span(c)[1], bank(2, 1 + n),
                           [("yb%d" % c, 2 * eng(partner, core)), act_t[(2, 1 + n)]])
        else:
            for j in range(2):
                for i in range(G):
                    mm_x(j, i)
            for j in range(K):
                run(j)
                if j + 2 < K:
                    for i in range(G):
                        mm_x(j + 2, i)
            y_part(T.hqA, T.hpA, 0, NC, T.ps[:, 0:NC], [hz[(rank, K - 1)], act_t[(2, 0)]])
        wait(SY, "sy", ("yst", cnt["yst"]))

    if paired:
        cut = cutting(core)
        for n in range(len(cut) - 1):
            wait(g, "g", qz[("w", n)])
            part = [p for p in pieces(core) if cut[n] <= p[0] < cut[n + 1]]
            for lo, hi, p in part:
                if p:
                    push(p[0], T.tp[:, lo:hi], T.wp[:, lo:hi], "tin")
            push(partner, T.w2q[:, cut[n]:cut[n + 1]].bitcast(dt.uint8), T.wq[:, cut[n]:cut[n + 1]].bitcast(dt.uint8), "pin")
            for lo, hi, p in part:
                if not p:
                    push(partner, T.w2p[:, lo:hi], T.wp[:, lo:hi], "pin")
        o = HW * (1 - own)
        wait(g, "g", qz[("x", 1 - own)])
        push_q(partner, T.x2q, T.x2p, T.xq, T.xp, o, o + HW, "pin")

    for s in ways:
        for lo, hi, p in ways[s]:
            if core in p:
                k = p.index(core)
                wait(g, "g", ("tin", eng(s if k == 0 else p[k - 1], core)))
                if k + 1 < len(p):
                    push(p[k + 1], T.tp[:, lo:hi], T.tp[:, lo:hi], "tin")
                else:
                    push([cores[r] for r in INNER if cores[r] != s][0], T.w2p[:, lo:hi], T.tp[:, lo:hi], "pin")

    for src, dst, c, cv, pv, L in hops:
        a, b = span(c)
        if core == src:
            hq, hp = OUT(L)[1:]
            wait(g, "g", hz[(L, c)])
            if cv is None:
                push_q(dst, T.iq, T.ip, hq, hp, a, b, "arr%d" % c)
            else:
                push(cv, T.rq[:, a:b].bitcast(dt.uint8), hq[:, a:b].bitcast(dt.uint8), "relc%d" % c)
                push(pv, T.rp[:, a:b], hp[:, a:b], "relp%d" % c)
        if core == cv:
            wait(g, "g", ("relc%d" % c, eng(src, cv)))
            push(dst, T.iq[:, a:b].bitcast(dt.uint8), T.rq[:, a:b].bitcast(dt.uint8), "arr%d" % c)
        if core == pv:
            wait(g, "g", ("relp%d" % c, eng(src, pv)))
            push(dst, T.ip[:, a:b], T.rp[:, a:b], "arr%d" % c)

    if paired:
        hq, hp = OUT(prank)[1:]
        if prank == nranks - 1:
            for c in (2 * fore, 2 * fore + 1):
                wait(g, "g", hz[(prank, c)])
                push_q(partner, T.yq, T.yp, hq, hp, span(c)[0], span(c)[1], "yb%d" % c)
        else:
            wait(g, "g", hz[(prank, 2 * fore + 1)])
            push_q(partner, T.yq, T.yp, hq, hp, HW * fore, HW * fore + HW, "yin")
    if cnt.get("sent", 0):
        wait(g, "g", ("sent", cnt["sent"]))
